import numpy as np
import ml_dtypes


def mxq(x, axis, fmt="e4m3"):
    dtype, down = {"e4m3": (ml_dtypes.float8_e4m3fn, 7), "e5m2": (ml_dtypes.float8_e5m2, 14)}[fmt]
    v = np.moveaxis(np.asarray(x, np.float32).astype(ml_dtypes.bfloat16).astype(np.float64), axis, -1)
    blocks = v.reshape(v.shape[:-1] + (-1, 32))
    amax = np.abs(blocks).max(-1, keepdims=True)
    byte = np.maximum(np.where(amax > 0, np.frexp(amax)[1] - 1 + 127, 0) - down, 1)
    scale = np.exp2(byte - 127.0)
    codes = (blocks / scale).astype(np.float32).astype(dtype).astype(np.float64)
    return np.moveaxis((codes * scale).reshape(v.shape), -1, axis)


WIDE = False


def mx_kscale(k):
    if not WIDE:
        return np.ones(k)
    levels = np.array([30, -30])
    if k % 512:
        return np.exp2(np.random.permutation(np.resize(levels, k // 32))).repeat(32)
    a = np.empty((k // 512, 16))
    for p in range(k // 512):
        a[p, :8] = np.random.permutation(np.resize(levels, 8))
        for g in range(8):
            far = levels[np.abs(levels - a[p, g]) >= 10]
            a[p, g + 8] = far[np.random.randint(len(far))]
    return np.exp2(a.ravel()).repeat(32)


def f64(x):
    return np.asarray(x).astype(np.float64)


def striped(idx):
    return np.tile(np.asarray(idx).reshape(-1, 16).T, (8, 1)).astype(np.uint16)


def unstriped(offs):
    return offs[:16].T.reshape(-1).astype(np.int64)


def striped8(idx):
    return np.asarray(idx).reshape(8, -1, 16).transpose(0, 2, 1).reshape(128, -1).astype(np.uint16)


def unstriped8(offs):
    return offs.reshape(8, 16, -1).transpose(0, 2, 1).reshape(8, -1).astype(np.int64)


def pick8(x, idx, run):
    r = np.arange(len(x))
    return x[r[:, None], idx[r % (8 * run) // run]]


E2M1 = np.array([0.0, 0.5, 1.0, 1.5, 2.0, 3.0, 4.0, 6.0, -0.0, -0.5, -1.0, -1.5, -2.0, -3.0, -4.0, -6.0])


def pack_weight(w, fmt):
    k, n = w.shape
    w = f64(np.asarray(w, np.float32).astype(ml_dtypes.bfloat16)).reshape(k // 32, 32, n)
    amax = np.abs(w).max(1)
    if fmt in ("e4m3", "e5m2"):
        byte = np.frexp(amax)[1] - 1 + 127 - (7 if fmt == "e4m3" else 14)
    else:
        mant, ex = np.frexp(amax / 6.0)
        byte = np.where(mant > 0.5, ex, ex - 1) + 127
    byte = np.clip(np.where(amax > 0, byte, 1), 1, 254)
    scaled = (w * np.exp2(127.0 - byte)[:, None, :]).reshape(k, n).astype(np.float32)
    by_word = np.ascontiguousarray(scaled.reshape(k // 512, 128, 4, n).transpose(0, 1, 3, 2))
    if fmt in ("e4m3", "e5m2"):
        words = by_word.astype(ml_dtypes.float8_e4m3fn if fmt == "e4m3" else ml_dtypes.float8_e5m2).view(np.uint8)
    else:
        c = by_word.astype(ml_dtypes.float4_e2m1fn).view(np.uint8) & 0xF
        words = (c[..., 0::2] | (c[..., 1::2] << 4)).reshape(k // 512, 128, 2 * n)
    return np.ascontiguousarray(words), np.ascontiguousarray(byte.astype(np.uint8).reshape(k // 512, 16, n))


def unpack_weight(words, scales, fmt):
    g, _, n = scales.shape
    words = np.ascontiguousarray(words).reshape(g, 128, n, -1)
    if fmt in ("e4m3", "e5m2"):
        vals = words.view(ml_dtypes.float8_e4m3fn if fmt == "e4m3" else ml_dtypes.float8_e5m2).astype(np.float64)
    else:
        nib = np.empty((g, 128, n, 4), np.uint8)
        nib[..., 0::2] = words & 0xF
        nib[..., 1::2] = words >> 4
        vals = E2M1[nib]
    vals = vals * np.repeat(np.exp2(scales.astype(np.float64) - 127.0), 8, axis=1)[..., None]
    return vals.transpose(0, 1, 3, 2).reshape(g * 512, n)


K, T, J, R, F, Z, O, U, D, N, S, E = 512, 1024, 256, 512, 512, 1024, 128, 128, 256, 256, 1024, 512


def setup_inputs():
    n = np.random.standard_normal
    idx = np.random.permutation(T)[:J]
    idx2 = np.random.permutation(Z)[:J]
    idx3 = np.stack([np.random.permutation(J)[:O] for _ in range(8)])
    idx4 = np.stack([np.random.permutation(J)[:U] for _ in range(8)])
    idx5 = np.random.permutation(S)[:N]
    idx6 = np.random.permutation(E)[:D]
    idx7 = np.random.permutation(E)[:D]
    ff = mx_kscale(F)
    fk = mx_kscale(K)
    fr = mx_kscale(R)
    xop = pack_weight(n((F, Z)) / ff[:, None], "e2m1")
    wp = pack_weight(n((K, R)) * 1 / np.sqrt(K) / fk[:, None] * fr, "e2m1")
    w2p = pack_weight(n((F, R)) * 1 / np.sqrt(F) * ff[:, None], "e5m2")
    vsp = pack_weight(n((R, S)) * 1 / np.sqrt(R) / fr[:, None], "e5m2")
    return {
        "xo_words": xop[0],
        "xo_scales": xop[1],
        "cq": (np.random.randint(-7, 8, (K, T)).astype(np.float64)).astype(np.float32),
        "gs": (np.random.uniform(0.1, 0.4, (K, 1)) * fk[:, None]).astype(np.float32),
        "w_words": wp[0],
        "w_scales": wp[1],
        "w2_words": w2p[0],
        "w2_scales": w2p[1],
        "vs_words": vsp[0],
        "vs_scales": vsp[1],
        "offs": striped(idx),
        "offs2": striped(idx2),
        "offs3": striped8(idx3),
        "offs4": striped8(idx4),
        "offs5": striped(idx5),
        "offs6": striped(idx6),
        "offs7": striped(idx7),
    }


def reference(xo_words, xo_scales, cq, gs, w_words, w_scales, w2_words, w2_scales, vs_words, vs_scales, offs, offs2, offs3, offs4, offs5, offs6, offs7):
    idx = unstriped(offs)
    idx2 = unstriped(offs2)
    idx3 = unstriped8(offs3)
    idx4 = unstriped8(offs4)
    idx5 = unstriped(offs5)
    idx6 = unstriped(offs6)
    idx7 = unstriped(offs7)
    xou = unpack_weight(xo_words, xo_scales, "e2m1")
    wu = unpack_weight(w_words, w_scales, "e2m1")
    w2u = unpack_weight(w2_words, w2_scales, "e5m2")
    vsu = unpack_weight(vs_words, vs_scales, "e5m2")
    x1 = f64(cq)[:, idx] * f64(gs)
    x1q = mxq(x1, 0, "e4m3")
    a = wu.T @ x1q
    xoidx2g = xou[:, idx2]
    b = w2u.T @ xoidx2g
    lb = b[:, 0:1]
    la = a[:, 0:1]
    h1 = pick8(a, idx3, 64) * lb
    h2 = pick8(b, idx4, 64) * la
    hid = np.concatenate([h1, h2], axis=1)
    vsidx5g = vsu[:, idx5]
    hidq = mxq(hid, 0, "e4m3")
    p = vsidx5g.T @ hidq
    pa = np.zeros((N, E))
    pa[:, idx6] = p
    pb = np.zeros((N, E))
    pb[:, idx7] = p
    y = pa + pb
    return y

@@ -1,0 +1,220 @@
+from contextlib import ExitStack
+
+import concourse.mybir as mybir
+
+K, T, J, R, F, Z, O, U, D, N, S, E = 512, 1024, 256, 512, 512, 1024, 128, 128, 256, 256, 1024, 512
+FLOPS = 2 * (K * R * J + F * R * J + R * N * D)
+
+F32 = mybir.dt.float32
+BF16 = mybir.dt.bfloat16
+I32 = mybir.dt.int32
+U32 = mybir.dt.uint32
+U16 = mybir.dt.uint16
+U8 = mybir.dt.uint8
+E4M3 = mybir.dt.float8_e4m3fn_x4
+E5M2 = mybir.dt.float8_e5m2_x4
+E2M1 = mybir.dt.float4_e2m1fn_x4
+COPY = mybir.ActivationFunctionType.Copy
+ADD = mybir.AluOpType.add
+
+P = 128
+PACK = 4
+QUADS = 4
+ALIGN = 64
+
+
+def tile_list_groupside_codednote_store_pagetwice_kernel(
+    tc, xo_words, xo_scales, cq, gs, w_words, w_scales, w2_words, w2_scales, vs_words, vs_scales,
+    offs, offs2, offs3, offs4, offs5, offs6, offs7, out,
+):
+    nc = tc.nc
+    with ExitStack() as ctx:
+        sb = ctx.enter_context(tc.tile_pool(name="sb", bufs=1))
+        shared = ctx.enter_context(tc.tile_pool(name="shared", bufs=1))
+        ps = ctx.enter_context(tc.psum_pool(name="ps", bufs=1))
+
+        def tile(name, shape, dtype):
+            return sb.tile(shape, dtype, name=name, align_bytes=ALIGN)
+
+        def load_list(name, src):
+            t = tile(name, list(src.shape), U16)
+            nc.sync.dma_start(t[:], src)
+            return t
+
+        def load_scale_rows(dst, src):
+            nc.sync.dma_start(out=dst, in_=src[0].bitcast(I32).rearrange("(q r) w -> r q w", r=4))
+
+        def spread(plane, staged):
+            for q in range(QUADS):
+                nc.vector.tensor_copy(out=plane[32 * q : 32 * q + 4, :].bitcast(I32), in_=staged[:, q, :])
+
+        def interleave_quantise(name, planes, cols):
+            woven = tile(name + "_woven", [P, cols * PACK], BF16)
+            nc.vector.tensor_copy(
+                out=woven[:].rearrange("p (c i t) -> p c t i", i=4, t=PACK),
+                in_=planes.rearrange("p t (c i) -> p c t i", i=4),
+            )
+            words = tile(name + "_words", [P, cols], U32)
+            scales = tile(name + "_scales", [P, cols], U8)
+            nc.vector.quantize_mx(out=words[:].bitcast(E4M3), scales=scales[:], in_=woven[:])
+            return words, scales
+
+        cq_rows = cq.rearrange("(p t) c -> t p c", t=PACK)
+        codes = [tile("codes%d" % t, [P, T], F32) for t in range(PACK - 1)]
+        codes.append(shared.tile([P, T], F32, name="codes_last", offset=0))
+        xo_staged = tile("xo_staged", [4, QUADS, Z // 4], I32)
+        load_scale_rows(xo_staged[:], xo_scales)
+        list2 = load_list("list2", offs2)
+        xo_all = tile("xo_all", [P, Z], U16)
+        nc.sync.dma_start(out=xo_all[:].bitcast(I32), in_=xo_words[0].bitcast(I32))
+        ww_staged = tile("ww_staged", [4, QUADS, 2 * R // 4], I32)
+        load_scale_rows(ww_staged[:, :, R // 4 :], w2_scales)
+        load_scale_rows(ww_staged[:, :, : R // 4], w_scales)
+        w2_raw = tile("w2_raw", [P, R], U32)
+        nc.sync.dma_start(out=w2_raw[:].bitcast(I32), in_=w2_words[0].rearrange("p n t -> p (n t)").bitcast(I32))
+        nc.sync.dma_start(out=codes[0][:], in_=cq_rows[0])
+        nc.sync.dma_start(out=codes[1][:], in_=cq_rows[1])
+        list1 = load_list("list1", offs)
+        steps = tile("steps", [P, PACK], F32)
+        nc.sync.dma_start(out=steps[:], in_=gs.rearrange("(p t) o -> p (t o)", t=PACK))
+        w_raw = tile("w_raw", [P, R], U16)
+        nc.sync.dma_start(out=w_raw[:].bitcast(I32), in_=w_words[0].bitcast(I32))
+        vs_staged = tile("vs_staged", [4, QUADS, S // 4], I32)
+        load_scale_rows(vs_staged[:], vs_scales)
+        list5 = load_list("list5", offs5)
+        nc.sync.dma_start(out=codes[2][:], in_=cq_rows[2])
+        nc.sync.dma_start(out=codes[3][:], in_=cq_rows[3])
+        list3 = load_list("list3", offs3)
+        list4 = load_list("list4", offs4)
+        vs_all = tile("vs_all", [P, S], U32)
+        nc.sync.dma_start(out=vs_all[:].bitcast(I32), in_=vs_words[0].rearrange("p n t -> p (n t)").bitcast(I32))
+        list6 = load_list("list6", offs6)
+        list7 = load_list("list7", offs7)
+
+        xo_plane = tile("xo_plane", [P, Z], U8)
+        ww_plane = tile("ww_plane", [P, 2 * R], U8)
+        vs_plane = tile("vs_plane", [P, S], U8)
+        for plane in (xo_plane, ww_plane, vs_plane):
+            nc.vector.memset(plane[:].bitcast(I32), 0)
+        pages = [[tile("page%d%d" % (l, m), [P, E], F32) for m in range(2)] for l in range(2)]
+        for l in range(2):
+            for m in range(2):
+                nc.vector.memset(pages[l][m][:], 0.0)
+
+        spread(xo_plane, xo_staged)
+        xo_s = tile("xo_s", [P, J], U8)
+        nc.vector.tensor_copy(out=xo_s[:], in_=xo_plane[:].indirect(list2[:]))
+        xo_g = tile("xo_g", [P, J], U16)
+        nc.vector.tensor_copy(out=xo_g[:], in_=xo_all[:].indirect(list2[:]))
+        spread(ww_plane, ww_staged)
+        ww_s = tile("ww_s", [P, 2 * R], U8)
+        nc.vector.tensor_copy(
+            out=ww_s[:].rearrange("p (g t m) -> p g t m", g=2, t=PACK),
+            in_=ww_plane[:].rearrange("p (g m t) -> p g t m", g=2, t=PACK),
+        )
+        w2_dealt = tile("w2_dealt", [P, R], U32)
+        nc.scalar.copy(
+            out=w2_dealt[:].rearrange("p (t m) -> p t m", t=PACK), in_=w2_raw[:].rearrange("p (m t) -> p t m", t=PACK)
+        )
+        w_dealt = tile("w_dealt", [P, R], U16)
+        nc.scalar.copy(
+            out=w_dealt[:].rearrange("p (t m) -> p t m", t=PACK), in_=w_raw[:].rearrange("p (m t) -> p t m", t=PACK)
+        )
+        b_banks = []
+        for half in range(2):
+            bank = ps.tile([P, 2, J], F32, name="b_bank%d" % half)
+            for i in range(2):
+                t = 2 * half + i
+                nc.tensor.matmul_mx(
+                    out=bank[:, i, :],
+                    lhsT=w2_dealt[:, t * P : (t + 1) * P].bitcast(E5M2),
+                    lhsT_scale=ww_s[:, R + t * P : R + (t + 1) * P],
+                    rhs=xo_g[:].bitcast(E2M1),
+                    rhs_scale=xo_s[:],
+                    start=True,
+                    stop=True,
+                )
+            b_banks.append(bank)
+
+        spread(vs_plane, vs_staged)
+        vs_s = tile("vs_s", [P, N], U8)
+        nc.vector.tensor_copy(out=vs_s[:], in_=vs_plane[:].indirect(list5[:]))
+
+        x1 = tile("x1", [P, PACK, J], BF16)
+        for t in range(PACK):
+            nc.scalar.activation(out=x1[:, t, :], in_=codes[t][:].indirect(list1[:]), func=COPY, scale=steps[:, t : t + 1])
+        b_tiles = []
+        for t in range(PACK):
+            bt = shared.tile([P, J], F32, name="b%d" % t, offset=4 * J * t)
+            nc.scalar.copy(out=bt[:], in_=b_banks[t // 2][:, t % 2, :])
+            b_tiles.append(bt)
+        x1_words, x1_scales = interleave_quantise("x1", x1[:], J)
+        a_banks = []
+        for t in range(PACK):
+            bank = ps.tile([P, J], F32, name="a_bank%d" % t)
+            nc.tensor.matmul_mx(
+                out=bank[:],
+                lhsT=w_dealt[:, t * P : (t + 1) * P].bitcast(E2M1),
+                lhsT_scale=ww_s[:, t * P : (t + 1) * P],
+                rhs=x1_words[:].bitcast(E4M3),
+                rhs_scale=x1_scales[:],
+                start=True,
+                stop=True,
+            )
+            a_banks.append(bank)
+        vs_g = tile("vs_g", [P, N], U32)
+        nc.vector.tensor_copy(out=vs_g[:], in_=vs_all[:].indirect(list5[:]))
+        a_tiles = []
+        for t in range(PACK):
+            at = tile("a%d" % t, [P, J], F32)
+            nc.vector.tensor_copy(out=at[:], in_=a_banks[t][:])
+            a_tiles.append(at)
+
+        halves = ((a_tiles, list3, b_tiles), (b_tiles, list4, a_tiles))
+        products = []
+        for h, (windows, places, factors) in enumerate(halves):
+            hid = tile("hid%d" % h, [P, PACK, O], BF16)
+            for t in range(PACK):
+                nc.scalar.activation(
+                    out=hid[:, t, :], in_=windows[t][:].indirect(places[:]), func=COPY, scale=factors[t][:, 0:1]
+                )
+            hid_words, hid_scales = interleave_quantise("hid%d" % h, hid[:], O)
+            bank = ps.tile([P, 2, O], F32, name="p_bank%d" % h)
+            for m in range(2):
+                nc.tensor.matmul_mx(
+                    out=bank[:, m, :],
+                    lhsT=vs_g[:, m * P : (m + 1) * P].bitcast(E5M2),
+                    lhsT_scale=vs_s[:, m * P : (m + 1) * P],
+                    rhs=hid_words[:].bitcast(E4M3),
+                    rhs_scale=hid_scales[:],
+                    start=True,
+                    stop=True,
+                )
+            prod = tile("prod%d" % h, [P, 2, O], F32)
+            products.append((prod, bank))
+
+        def put(engine, l, m, d0, d1):
+            prod = products[d0 // O][0]
+            window = pages[l][m][:].indirect((list6, list7)[l][:, d0 // 16 : d1 // 16])
+            src = prod[:, m, d0 % O : d0 % O + d1 - d0]
+            if engine == "vector":
+                nc.vector.tensor_copy(out=window, in_=src)
+            else:
+                nc.scalar.activation(out=window, in_=src, func=COPY)
+
+        def add_store(m):
+            total = tile("total%d" % m, [P, E], F32)
+            nc.vector.tensor_tensor(out=total[:], in0=pages[0][m][:], in1=pages[1][m][:], op=ADD)
+            nc.sync.dma_start(out=out[m * P : (m + 1) * P, :], in_=total[:])
+
+        for h in range(2):
+            nc.scalar.copy(out=products[h][0][:], in_=products[h][1][:])
+            put("vector", 0, 0, h * O, (h + 1) * O)
+            put("scalar", 1, 0, h * O, (h + 1) * O)
+        put("scalar", 0, 1, 0, 64)
+        add_store(0)
+        put("scalar", 1, 1, 0, O)
+        put("scalar", 1, 1, O, D)
+        put("vector", 0, 1, 64, O)
+        put("vector", 0, 1, O, D)
+        add_store(1)

@@ -21,6 +21,7 @@ P = 128
 PACK = 4
 QUADS = 4
 ALIGN = 64
+LA_AT = 4 * T
 
 
 def tile_list_groupside_codednote_store_pagetwice_kernel(
@@ -48,20 +49,17 @@ def tile_list_groupside_codednote_store_pagetwice_kernel(
             for q in range(QUADS):
                 nc.vector.tensor_copy(out=plane[32 * q : 32 * q + 4, :].bitcast(I32), in_=staged[:, q, :])
 
-        def interleave_quantise(name, planes, cols):
+        def interleave_quantise(name, planes, cols, words, scales):
             woven = tile(name + "_woven", [P, cols * PACK], BF16)
             nc.vector.tensor_copy(
                 out=woven[:].rearrange("p (c i t) -> p c t i", i=4, t=PACK),
                 in_=planes.rearrange("p t (c i) -> p c t i", i=4),
             )
-            words = tile(name + "_words", [P, cols], U32)
-            scales = tile(name + "_scales", [P, cols], U8)
             nc.vector.quantize_mx(out=words[:].bitcast(E4M3), scales=scales[:], in_=woven[:])
-            return words, scales
 
         cq_rows = cq.rearrange("(p t) c -> t p c", t=PACK)
         codes = [tile("codes%d" % t, [P, T], F32) for t in range(PACK - 1)]
-        codes.append(shared.tile([P, T], F32, name="codes_last", offset=0))
+        codes.append(shared.tile([P, T], F32, name="codes_last", offset=0, align_bytes=ALIGN))
         xo_staged = tile("xo_staged", [4, QUADS, Z // 4], I32)
         load_scale_rows(xo_staged[:], xo_scales)
         list2 = load_list("list2", offs2)
@@ -122,7 +120,7 @@ def tile_list_groupside_codednote_store_pagetwice_kernel(
         )
         b_banks = []
         for half in range(2):
-            bank = ps.tile([P, 2, J], F32, name="b_bank%d" % half)
+            bank = ps.tile([P, 2, J], F32, name="b_bank%d" % half, tag="pair_bank%d" % half)
             for i in range(2):
                 t = 2 * half + i
                 nc.tensor.matmul_mx(
@@ -145,10 +143,12 @@ def tile_list_groupside_codednote_store_pagetwice_kernel(
             nc.scalar.activation(out=x1[:, t, :], in_=codes[t][:].indirect(list1[:]), func=COPY, scale=steps[:, t : t + 1])
         b_tiles = []
         for t in range(PACK):
-            bt = shared.tile([P, J], F32, name="b%d" % t, offset=4 * J * t)
+            bt = shared.tile([P, J], F32, name="b%d" % t, offset=4 * J * t, align_bytes=ALIGN)
             nc.scalar.copy(out=bt[:], in_=b_banks[t // 2][:, t % 2, :])
             b_tiles.append(bt)
-        x1_words, x1_scales = interleave_quantise("x1", x1[:], J)
+        x1_words = tile("x1_words", [P, J], U32)
+        x1_scales = tile("x1_scales", [P, J], U8)
+        interleave_quantise("x1", x1[:], J, x1_words, x1_scales)
         a_banks = []
         for t in range(PACK):
             bank = ps.tile([P, J], F32, name="a_bank%d" % t)
@@ -164,25 +164,36 @@ def tile_list_groupside_codednote_store_pagetwice_kernel(
             a_banks.append(bank)
         vs_g = tile("vs_g", [P, N], U32)
         nc.vector.tensor_copy(out=vs_g[:], in_=vs_all[:].indirect(list5[:]))
+        la = shared.tile([P, PACK], F32, name="la", offset=LA_AT, align_bytes=ALIGN)
         a_tiles = []
         for t in range(PACK):
+            nc.vector.tensor_copy(out=la[:, t : t + 1], in_=a_banks[t][:, 0:1])
             at = tile("a%d" % t, [P, J], F32)
             nc.vector.tensor_copy(out=at[:], in_=a_banks[t][:])
             a_tiles.append(at)
 
-        halves = ((a_tiles, list3, b_tiles), (b_tiles, list4, a_tiles))
+        halves = (
+            (b_tiles, list4, [la[:, t : t + 1] for t in range(PACK)]),
+            (a_tiles, list3, [b_tiles[t][:, 0:1] for t in range(PACK)]),
+        )
         products = []
         for h, (windows, places, factors) in enumerate(halves):
-            hid = tile("hid%d" % h, [P, PACK, O], BF16)
+            hid = shared.tile([P, PACK, O], BF16, name="hid%d" % h, offset=LA_AT + (1 - h) * 2 * PACK * O, align_bytes=ALIGN)
             for t in range(PACK):
                 nc.scalar.activation(
-                    out=hid[:, t, :], in_=windows[t][:].indirect(places[:]), func=COPY, scale=factors[t][:, 0:1]
+                    out=hid[:, t, :], in_=windows[t][:].indirect(places[:]), func=COPY, scale=factors[t]
                 )
-            hid_words, hid_scales = interleave_quantise("hid%d" % h, hid[:], O)
-            bank = ps.tile([P, 2, O], F32, name="p_bank%d" % h)
+            hid_words = tile("hid%d_words" % h, [P, O], U32)
+            hid_scales = tile("hid%d_scales" % h, [P, O], U8)
+            interleave_quantise("hid%d" % h, hid[:], O, hid_words, hid_scales)
+            if h == 0:
+                banks = [ps.tile([P, O], F32, name="p_bank%d" % m)[:] for m in range(2)]
+            else:
+                bank = ps.tile([P, 2, O], F32, name="p_last", tag="pair_bank0")
+                banks = [bank[:, m, :] for m in range(2)]
             for m in range(2):
                 nc.tensor.matmul_mx(
-                    out=bank[:, m, :],
+                    out=banks[m],
                     lhsT=vs_g[:, m * P : (m + 1) * P].bitcast(E5M2),
                     lhsT_scale=vs_s[:, m * P : (m + 1) * P],
                     rhs=hid_words[:].bitcast(E4M3),
@@ -191,30 +202,34 @@ def tile_list_groupside_codednote_store_pagetwice_kernel(
                     stop=True,
                 )
             prod = tile("prod%d" % h, [P, 2, O], F32)
-            products.append((prod, bank))
+            products.append((prod, banks if h == 0 else bank))
 
         def put(engine, l, m, d0, d1):
             prod = products[d0 // O][0]
-            window = pages[l][m][:].indirect((list6, list7)[l][:, d0 // 16 : d1 // 16])
+            e0 = (d0 + O) % D
+            window = pages[l][m][:].indirect((list6, list7)[l][:, e0 // 16 : (e0 + d1 - d0) // 16])
             src = prod[:, m, d0 % O : d0 % O + d1 - d0]
             if engine == "vector":
                 nc.vector.tensor_copy(out=window, in_=src)
             else:
                 nc.scalar.activation(out=window, in_=src, func=COPY)
 
-        def add_store(m):
-            total = tile("total%d" % m, [P, E], F32)
-            nc.vector.tensor_tensor(out=total[:], in0=pages[0][m][:], in1=pages[1][m][:], op=ADD)
-            nc.sync.dma_start(out=out[m * P : (m + 1) * P, :], in_=total[:])
+        def add_store(m, e0, e1):
+            total = tile("total%d_%d" % (m, e0), [P, e1 - e0], F32)
+            nc.vector.tensor_tensor(out=total[:], in0=pages[0][m][:, e0:e1], in1=pages[1][m][:, e0:e1], op=ADD)
+            nc.sync.dma_start(out=out[m * P : (m + 1) * P, e0:e1], in_=total[:])
 
-        for h in range(2):
-            nc.scalar.copy(out=products[h][0][:], in_=products[h][1][:])
-            put("vector", 0, 0, h * O, (h + 1) * O)
-            put("scalar", 1, 0, h * O, (h + 1) * O)
-        put("scalar", 0, 1, 0, 64)
-        add_store(0)
+        nc.scalar.copy(out=products[0][0][:, 0, :], in_=products[0][1][0])
+        put("vector", 0, 0, 0, O)
+        put("scalar", 1, 0, 0, O)
+        nc.scalar.copy(out=products[0][0][:, 1, :], in_=products[0][1][1])
+        put("scalar", 0, 1, 0, O)
+        nc.vector.tensor_copy(out=products[1][0][:], in_=products[1][1][:])
+        put("vector", 0, 0, O, D)
+        put("scalar", 1, 0, O, D)
+        put("vector", 0, 1, O, D)
+        add_store(0, 0, E)
         put("scalar", 1, 1, 0, O)
         put("scalar", 1, 1, O, D)
-        put("vector", 0, 1, 64, O)
-        put("vector", 0, 1, O, D)
-        add_store(1)
+        add_store(1, 0, E // 2)
+        add_store(1, E // 2, E)

@@ -73,15 +73,15 @@ def tile_list_groupside_codednote_store_pagetwice_kernel(
         nc.sync.dma_start(out=codes[0][:], in_=cq_rows[0])
         nc.sync.dma_start(out=codes[1][:], in_=cq_rows[1])
         list1 = load_list("list1", offs)
-        steps = tile("steps", [P, PACK], F32)
+        steps = shared.tile([P, PACK], F32, name="steps", offset=LA_AT, align_bytes=ALIGN)
         nc.sync.dma_start(out=steps[:], in_=gs.rearrange("(p t) o -> p (t o)", t=PACK))
-        w_raw = tile("w_raw", [P, R], U16)
-        nc.sync.dma_start(out=w_raw[:].bitcast(I32), in_=w_words[0].bitcast(I32))
         vs_staged = tile("vs_staged", [4, QUADS, S // 4], I32)
         load_scale_rows(vs_staged[:], vs_scales)
         list5 = load_list("list5", offs5)
         nc.sync.dma_start(out=codes[2][:], in_=cq_rows[2])
         nc.sync.dma_start(out=codes[3][:], in_=cq_rows[3])
+        w_raw = tile("w_raw", [P, R], U16)
+        nc.sync.dma_start(out=w_raw[:].bitcast(I32), in_=w_words[0].bitcast(I32))
         list3 = load_list("list3", offs3)
         list4 = load_list("list4", offs4)
         vs_all = tile("vs_all", [P, S], U32)
@@ -114,10 +114,6 @@ def tile_list_groupside_codednote_store_pagetwice_kernel(
         nc.scalar.copy(
             out=w2_dealt[:].rearrange("p (t m) -> p t m", t=PACK), in_=w2_raw[:].rearrange("p (m t) -> p t m", t=PACK)
         )
-        w_dealt = tile("w_dealt", [P, R], U16)
-        nc.scalar.copy(
-            out=w_dealt[:].rearrange("p (t m) -> p t m", t=PACK), in_=w_raw[:].rearrange("p (m t) -> p t m", t=PACK)
-        )
         b_banks = []
         for half in range(2):
             bank = ps.tile([P, 2, J], F32, name="b_bank%d" % half, tag="pair_bank%d" % half)
@@ -138,9 +134,16 @@ def tile_list_groupside_codednote_store_pagetwice_kernel(
         vs_s = tile("vs_s", [P, N], U8)
         nc.vector.tensor_copy(out=vs_s[:], in_=vs_plane[:].indirect(list5[:]))
 
+        w_dealt = tile("w_dealt", [P, R], U16)
+        nc.vector.tensor_copy(
+            out=w_dealt[:].rearrange("p (t m) -> p t m", t=PACK), in_=w_raw[:].rearrange("p (m t) -> p t m", t=PACK)
+        )
         x1 = tile("x1", [P, PACK, J], BF16)
         for t in range(PACK):
             nc.scalar.activation(out=x1[:, t, :], in_=codes[t][:].indirect(list1[:]), func=COPY, scale=steps[:, t : t + 1])
+        lb = shared.tile([P, PACK], F32, name="lb", offset=LA_AT, align_bytes=ALIGN)
+        for half in range(2):
+            nc.scalar.copy(out=lb[:, 2 * half : 2 * half + 2], in_=b_banks[half][:, :, 0])
         b_tiles = []
         for t in range(PACK):
             bt = shared.tile([P, J], F32, name="b%d" % t, offset=4 * J * t, align_bytes=ALIGN)
@@ -164,17 +167,18 @@ def tile_list_groupside_codednote_store_pagetwice_kernel(
             a_banks.append(bank)
         vs_g = tile("vs_g", [P, N], U32)
         nc.vector.tensor_copy(out=vs_g[:], in_=vs_all[:].indirect(list5[:]))
-        la = shared.tile([P, PACK], F32, name="la", offset=LA_AT, align_bytes=ALIGN)
         a_tiles = []
         for t in range(PACK):
-            nc.vector.tensor_copy(out=la[:, t : t + 1], in_=a_banks[t][:, 0:1])
             at = tile("a%d" % t, [P, J], F32)
-            nc.vector.tensor_copy(out=at[:], in_=a_banks[t][:])
+            if t == 0:
+                nc.scalar.copy(out=at[:], in_=a_banks[t][:])
+            else:
+                nc.vector.tensor_copy(out=at[:], in_=a_banks[t][:])
             a_tiles.append(at)
 
         halves = (
-            (b_tiles, list4, [la[:, t : t + 1] for t in range(PACK)]),
-            (a_tiles, list3, [b_tiles[t][:, 0:1] for t in range(PACK)]),
+            (a_tiles, list3, [lb[:, t : t + 1] for t in range(PACK)]),
+            (b_tiles, list4, [a_tiles[t][:, 0:1] for t in range(PACK)]),
         )
         products = []
         for h, (windows, places, factors) in enumerate(halves):
@@ -201,14 +205,18 @@ def tile_list_groupside_codednote_store_pagetwice_kernel(
                     start=True,
                     stop=True,
                 )
-            prod = tile("prod%d" % h, [P, 2, O], F32)
-            products.append((prod, banks if h == 0 else bank))
+            if h == 0:
+                first = shared.tile([P, O], F32, name="prod00", offset=4 * J * (PACK - 1), align_bytes=ALIGN)
+                prod = [first[:], tile("prod01", [P, O], F32)[:]]
+                products.append((prod, banks))
+            else:
+                last = tile("prod1", [P, 2, O], F32)
+                products.append(([last[:, m, :] for m in range(2)], bank))
 
         def put(engine, l, m, d0, d1):
             prod = products[d0 // O][0]
-            e0 = (d0 + O) % D
-            window = pages[l][m][:].indirect((list6, list7)[l][:, e0 // 16 : (e0 + d1 - d0) // 16])
-            src = prod[:, m, d0 % O : d0 % O + d1 - d0]
+            window = pages[l][m][:].indirect((list6, list7)[l][:, d0 // 16 : d1 // 16])
+            src = prod[m][:, d0 % O : d0 % O + d1 - d0]
             if engine == "vector":
                 nc.vector.tensor_copy(out=window, in_=src)
             else:
@@ -219,17 +227,17 @@ def tile_list_groupside_codednote_store_pagetwice_kernel(
             nc.vector.tensor_tensor(out=total[:], in0=pages[0][m][:, e0:e1], in1=pages[1][m][:, e0:e1], op=ADD)
             nc.sync.dma_start(out=out[m * P : (m + 1) * P, e0:e1], in_=total[:])
 
-        nc.scalar.copy(out=products[0][0][:, 0, :], in_=products[0][1][0])
-        put("vector", 0, 0, 0, O)
+        nc.scalar.copy(out=products[0][0][0], in_=products[0][1][0])
+        nc.vector.tensor_copy(out=products[0][0][1], in_=products[0][1][1])
+        put("scalar", 0, 0, 0, O)
+        put("vector", 0, 1, 0, O)
         put("scalar", 1, 0, 0, O)
-        nc.scalar.copy(out=products[0][0][:, 1, :], in_=products[0][1][1])
-        put("scalar", 0, 1, 0, O)
-        nc.vector.tensor_copy(out=products[1][0][:], in_=products[1][1][:])
+        nc.vector.tensor_copy(out=last[:], in_=products[1][1][:])
         put("vector", 0, 0, O, D)
+        put("scalar", 1, 1, 0, O)
         put("scalar", 1, 0, O, D)
         put("vector", 0, 1, O, D)
         add_store(0, 0, E)
-        put("scalar", 1, 1, 0, O)
         put("scalar", 1, 1, O, D)
         add_store(1, 0, E // 2)
         add_store(1, E // 2, E)

from contextlib import ExitStack

import concourse.mybir as mybir

K, T, J, R, F, Z, O, U, D, N, S, E = 512, 1024, 256, 512, 512, 1024, 128, 128, 256, 256, 1024, 512
FLOPS = 2 * (K * R * J + F * R * J + R * N * D)

F32 = mybir.dt.float32
BF16 = mybir.dt.bfloat16
I32 = mybir.dt.int32
U32 = mybir.dt.uint32
U16 = mybir.dt.uint16
U8 = mybir.dt.uint8
E4M3 = mybir.dt.float8_e4m3fn_x4
E5M2 = mybir.dt.float8_e5m2_x4
E2M1 = mybir.dt.float4_e2m1fn_x4
COPY = mybir.ActivationFunctionType.Copy
ADD = mybir.AluOpType.add

P = 128
PACK = 4
QUADS = 4
ALIGN = 64
LA_AT = 4 * T


def tile_list_groupside_codednote_store_pagetwice_kernel(
    tc, xo_words, xo_scales, cq, gs, w_words, w_scales, w2_words, w2_scales, vs_words, vs_scales,
    offs, offs2, offs3, offs4, offs5, offs6, offs7, out,
):
    nc = tc.nc
    with ExitStack() as ctx:
        sb = ctx.enter_context(tc.tile_pool(name="sb", bufs=1))
        shared = ctx.enter_context(tc.tile_pool(name="shared", bufs=1))
        ps = ctx.enter_context(tc.psum_pool(name="ps", bufs=1))

        def tile(name, shape, dtype):
            return sb.tile(shape, dtype, name=name, align_bytes=ALIGN)

        def load_list(name, src):
            t = tile(name, list(src.shape), U16)
            nc.sync.dma_start(t[:], src)
            return t

        def load_scale_rows(dst, src):
            nc.sync.dma_start(out=dst, in_=src[0].bitcast(I32).rearrange("(q r) w -> r q w", r=4))

        def spread(plane, staged):
            for q in range(QUADS):
                nc.vector.tensor_copy(out=plane[32 * q : 32 * q + 4, :].bitcast(I32), in_=staged[:, q, :])

        def interleave_quantise(name, planes, cols, words, scales):
            woven = tile(name + "_woven", [P, cols * PACK], BF16)
            nc.vector.tensor_copy(
                out=woven[:].rearrange("p (c i t) -> p c t i", i=4, t=PACK),
                in_=planes.rearrange("p t (c i) -> p c t i", i=4),
            )
            nc.vector.quantize_mx(out=words[:].bitcast(E4M3), scales=scales[:], in_=woven[:])

        cq_rows = cq.rearrange("(p t) c -> t p c", t=PACK)
        codes = [tile("codes%d" % t, [P, T], F32) for t in range(PACK - 1)]
        codes.append(shared.tile([P, T], F32, name="codes_last", offset=0, align_bytes=ALIGN))
        xo_staged = tile("xo_staged", [4, QUADS, Z // 4], I32)
        load_scale_rows(xo_staged[:], xo_scales)
        list2 = load_list("list2", offs2)
        xo_all = tile("xo_all", [P, Z], U16)
        nc.sync.dma_start(out=xo_all[:].bitcast(I32), in_=xo_words[0].bitcast(I32))
        ww_staged = tile("ww_staged", [4, QUADS, 2 * R // 4], I32)
        load_scale_rows(ww_staged[:, :, R // 4 :], w2_scales)
        load_scale_rows(ww_staged[:, :, : R // 4], w_scales)
        w2_raw = tile("w2_raw", [P, R], U32)
        nc.sync.dma_start(out=w2_raw[:].bitcast(I32), in_=w2_words[0].rearrange("p n t -> p (n t)").bitcast(I32))
        nc.sync.dma_start(out=codes[0][:], in_=cq_rows[0])
        nc.sync.dma_start(out=codes[1][:], in_=cq_rows[1])
        list1 = load_list("list1", offs)
        steps = shared.tile([P, PACK], F32, name="steps", offset=LA_AT, align_bytes=ALIGN)
        nc.sync.dma_start(out=steps[:], in_=gs.rearrange("(p t) o -> p (t o)", t=PACK))
        vs_staged = tile("vs_staged", [4, QUADS, S // 4], I32)
        load_scale_rows(vs_staged[:], vs_scales)
        list5 = load_list("list5", offs5)
        nc.sync.dma_start(out=codes[2][:], in_=cq_rows[2])
        nc.sync.dma_start(out=codes[3][:], in_=cq_rows[3])
        w_raw = tile("w_raw", [P, R], U16)
        nc.sync.dma_start(out=w_raw[:].bitcast(I32), in_=w_words[0].bitcast(I32))
        list3 = load_list("list3", offs3)
        list4 = load_list("list4", offs4)
        vs_all = tile("vs_all", [P, S], U32)
        nc.sync.dma_start(out=vs_all[:].bitcast(I32), in_=vs_words[0].rearrange("p n t -> p (n t)").bitcast(I32))
        list6 = load_list("list6", offs6)
        list7 = load_list("list7", offs7)

        xo_plane = tile("xo_plane", [P, Z], U8)
        ww_plane = tile("ww_plane", [P, 2 * R], U8)
        vs_plane = tile("vs_plane", [P, S], U8)
        for plane in (xo_plane, ww_plane, vs_plane):
            nc.vector.memset(plane[:].bitcast(I32), 0)
        pages = [[tile("page%d%d" % (l, m), [P, E], F32) for m in range(2)] for l in range(2)]
        for l in range(2):
            for m in range(2):
                nc.vector.memset(pages[l][m][:], 0.0)

        spread(xo_plane, xo_staged)
        xo_s = tile("xo_s", [P, J], U8)
        nc.vector.tensor_copy(out=xo_s[:], in_=xo_plane[:].indirect(list2[:]))
        xo_g = tile("xo_g", [P, J], U16)
        nc.vector.tensor_copy(out=xo_g[:], in_=xo_all[:].indirect(list2[:]))
        spread(ww_plane, ww_staged)
        ww_s = tile("ww_s", [P, 2 * R], U8)
        nc.vector.tensor_copy(
            out=ww_s[:].rearrange("p (g t m) -> p g t m", g=2, t=PACK),
            in_=ww_plane[:].rearrange("p (g m t) -> p g t m", g=2, t=PACK),
        )
        w2_dealt = tile("w2_dealt", [P, R], U32)
        nc.scalar.copy(
            out=w2_dealt[:].rearrange("p (t m) -> p t m", t=PACK), in_=w2_raw[:].rearrange("p (m t) -> p t m", t=PACK)
        )
        b_banks = []
        for half in range(2):
            bank = ps.tile([P, 2, J], F32, name="b_bank%d" % half, tag="pair_bank%d" % half)
            for i in range(2):
                t = 2 * half + i
                nc.tensor.matmul_mx(
                    out=bank[:, i, :],
                    lhsT=w2_dealt[:, t * P : (t + 1) * P].bitcast(E5M2),
                    lhsT_scale=ww_s[:, R + t * P : R + (t + 1) * P],
                    rhs=xo_g[:].bitcast(E2M1),
                    rhs_scale=xo_s[:],
                    start=True,
                    stop=True,
                )
            b_banks.append(bank)

        spread(vs_plane, vs_staged)
        vs_s = tile("vs_s", [P, N], U8)
        nc.vector.tensor_copy(out=vs_s[:], in_=vs_plane[:].indirect(list5[:]))

        w_dealt = tile("w_dealt", [P, R], U16)
        nc.vector.tensor_copy(
            out=w_dealt[:].rearrange("p (t m) -> p t m", t=PACK), in_=w_raw[:].rearrange("p (m t) -> p t m", t=PACK)
        )
        x1 = tile("x1", [P, PACK, J], BF16)
        for t in range(PACK):
            nc.scalar.activation(out=x1[:, t, :], in_=codes[t][:].indirect(list1[:]), func=COPY, scale=steps[:, t : t + 1])
        lb = shared.tile([P, PACK], F32, name="lb", offset=LA_AT, align_bytes=ALIGN)
        for half in range(2):
            nc.scalar.copy(out=lb[:, 2 * half : 2 * half + 2], in_=b_banks[half][:, :, 0])
        b_tiles = []
        for t in range(PACK):
            bt = shared.tile([P, J], F32, name="b%d" % t, offset=4 * J * t, align_bytes=ALIGN)
            nc.scalar.copy(out=bt[:], in_=b_banks[t // 2][:, t % 2, :])
            b_tiles.append(bt)
        x1_words = tile("x1_words", [P, J], U32)
        x1_scales = tile("x1_scales", [P, J], U8)
        interleave_quantise("x1", x1[:], J, x1_words, x1_scales)
        a_banks = []
        for t in range(PACK):
            bank = ps.tile([P, J], F32, name="a_bank%d" % t)
            nc.tensor.matmul_mx(
                out=bank[:],
                lhsT=w_dealt[:, t * P : (t + 1) * P].bitcast(E2M1),
                lhsT_scale=ww_s[:, t * P : (t + 1) * P],
                rhs=x1_words[:].bitcast(E4M3),
                rhs_scale=x1_scales[:],
                start=True,
                stop=True,
            )
            a_banks.append(bank)
        vs_g = tile("vs_g", [P, N], U32)
        nc.vector.tensor_copy(out=vs_g[:], in_=vs_all[:].indirect(list5[:]))
        a_tiles = []
        for t in range(PACK):
            at = tile("a%d" % t, [P, J], F32)
            if t == 0:
                nc.scalar.copy(out=at[:], in_=a_banks[t][:])
            else:
                nc.vector.tensor_copy(out=at[:], in_=a_banks[t][:])
            a_tiles.append(at)

        halves = (
            (a_tiles, list3, [lb[:, t : t + 1] for t in range(PACK)]),
            (b_tiles, list4, [a_tiles[t][:, 0:1] for t in range(PACK)]),
        )
        products = []
        for h, (windows, places, factors) in enumerate(halves):
            hid = shared.tile([P, PACK, O], BF16, name="hid%d" % h, offset=LA_AT + (1 - h) * 2 * PACK * O, align_bytes=ALIGN)
            for t in range(PACK):
                nc.scalar.activation(
                    out=hid[:, t, :], in_=windows[t][:].indirect(places[:]), func=COPY, scale=factors[t]
                )
            hid_words = tile("hid%d_words" % h, [P, O], U32)
            hid_scales = tile("hid%d_scales" % h, [P, O], U8)
            interleave_quantise("hid%d" % h, hid[:], O, hid_words, hid_scales)
            if h == 0:
                banks = [ps.tile([P, O], F32, name="p_bank%d" % m)[:] for m in range(2)]
            else:
                bank = ps.tile([P, 2, O], F32, name="p_last", tag="pair_bank0")
                banks = [bank[:, m, :] for m in range(2)]
            for m in range(2):
                nc.tensor.matmul_mx(
                    out=banks[m],
                    lhsT=vs_g[:, m * P : (m + 1) * P].bitcast(E5M2),
                    lhsT_scale=vs_s[:, m * P : (m + 1) * P],
                    rhs=hid_words[:].bitcast(E4M3),
                    rhs_scale=hid_scales[:],
                    start=True,
                    stop=True,
                )
            if h == 0:
                first = shared.tile([P, O], F32, name="prod00", offset=4 * J * (PACK - 1), align_bytes=ALIGN)
                prod = [first[:], tile("prod01", [P, O], F32)[:]]
                products.append((prod, banks))
            else:
                last = tile("prod1", [P, 2, O], F32)
                products.append(([last[:, m, :] for m in range(2)], bank))

        def put(engine, l, m, d0, d1):
            prod = products[d0 // O][0]
            window = pages[l][m][:].indirect((list6, list7)[l][:, d0 // 16 : d1 // 16])
            src = prod[m][:, d0 % O : d0 % O + d1 - d0]
            if engine == "vector":
                nc.vector.tensor_copy(out=window, in_=src)
            else:
                nc.scalar.activation(out=window, in_=src, func=COPY)

        def add_store(m, e0, e1):
            total = tile("total%d_%d" % (m, e0), [P, e1 - e0], F32)
            nc.vector.tensor_tensor(out=total[:], in0=pages[0][m][:, e0:e1], in1=pages[1][m][:, e0:e1], op=ADD)
            nc.sync.dma_start(out=out[m * P : (m + 1) * P, e0:e1], in_=total[:])

        nc.scalar.copy(out=products[0][0][0], in_=products[0][1][0])
        nc.vector.tensor_copy(out=products[0][0][1], in_=products[0][1][1])
        put("scalar", 0, 0, 0, O)
        put("vector", 0, 1, 0, O)
        put("scalar", 1, 0, 0, O)
        nc.vector.tensor_copy(out=last[:], in_=products[1][1][:])
        put("vector", 0, 0, O, D)
        put("scalar", 1, 1, 0, O)
        put("scalar", 1, 0, O, D)
        put("vector", 0, 1, O, D)
        add_store(0, 0, E)
        put("scalar", 1, 1, O, D)
        add_store(1, 0, E // 2)
        add_store(1, E // 2, E)
